import numpy as np
import ml_dtypes


def mxq(x, axis, fmt="e4m3"):
    dtype, down = {"e4m3": (ml_dtypes.float8_e4m3fn, 7), "e5m2": (ml_dtypes.float8_e5m2, 14)}[fmt]
    v = np.moveaxis(np.asarray(x, np.float32).astype(ml_dtypes.bfloat16).astype(np.float64), axis, -1)
    blocks = v.reshape(v.shape[:-1] + (-1, 32))
    amax = np.abs(blocks).max(-1, keepdims=True)
    byte = np.maximum(np.where(amax > 0, np.frexp(amax)[1] - 1 + 127, 0) - down, 1)
    scale = np.exp2(byte - 127.0)
    codes = (blocks / scale).astype(np.float32).astype(dtype).astype(np.float64)
    return np.moveaxis((codes * scale).reshape(v.shape), -1, axis)


WIDE = False


def mx_kscale(k):
    if not WIDE:
        return np.ones(k)
    levels = np.array([10, -10, 5, -5, 0])
    if k % 512:
        return np.exp2(np.random.permutation(np.resize(levels, k // 32))).repeat(32)
    a = np.empty((k // 512, 16))
    for p in range(k // 512):
        a[p, :8] = np.random.permutation(np.resize(levels, 8))
        for g in range(8):
            far = levels[np.abs(levels - a[p, g]) >= 10]
            a[p, g + 8] = far[np.random.randint(len(far))]
    return np.exp2(a.ravel()).repeat(32)


def f64(x):
    return np.asarray(x).astype(np.float64)


def striped(idx):
    return np.tile(idx.reshape(-1, 16).T, (8, 1)).astype(np.uint16)


def unstriped(offs):
    return offs[:16].T.reshape(-1).astype(np.int64)


E2M1 = np.array([0.0, 0.5, 1.0, 1.5, 2.0, 3.0, 4.0, 6.0, -0.0, -0.5, -1.0, -1.5, -2.0, -3.0, -4.0, -6.0])


def pack_weight(w, fmt):
    k, n = w.shape
    w = f64(np.asarray(w, np.float32).astype(ml_dtypes.bfloat16)).reshape(k // 32, 32, n)
    amax = np.abs(w).max(1)
    if fmt == "e4m3":
        byte = np.frexp(amax)[1] - 1 + 127 - 7
    else:
        mant, ex = np.frexp(amax / 6.0)
        byte = np.where(mant > 0.5, ex, ex - 1) + 127
    byte = np.clip(np.where(amax > 0, byte, 1), 1, 254)
    scaled = (w * np.exp2(127.0 - byte)[:, None, :]).reshape(k, n).astype(np.float32)
    by_word = np.ascontiguousarray(scaled.reshape(k // 512, 128, 4, n).transpose(0, 1, 3, 2))
    if fmt == "e4m3":
        words = by_word.astype(ml_dtypes.float8_e4m3fn).view(np.uint8)
    else:
        c = by_word.astype(ml_dtypes.float4_e2m1fn).view(np.uint8) & 0xF
        words = (c[..., 0::2] | (c[..., 1::2] << 4)).reshape(k // 512, 128, 2 * n)
    return np.ascontiguousarray(words), np.ascontiguousarray(byte.astype(np.uint8).reshape(k // 512, 16, n))


def unpack_weight(words, scales, fmt):
    g, _, n = scales.shape
    words = np.ascontiguousarray(words).reshape(g, 128, n, -1)
    if fmt == "e4m3":
        vals = words.view(ml_dtypes.float8_e4m3fn).astype(np.float64)
    else:
        nib = np.empty((g, 128, n, 4), np.uint8)
        nib[..., 0::2] = words & 0xF
        nib[..., 1::2] = words >> 4
        vals = E2M1[nib]
    vals = vals * np.repeat(np.exp2(scales.astype(np.float64) - 127.0), 8, axis=1)[..., None]
    return vals.transpose(0, 1, 3, 2).reshape(g * 512, n)


def gelu(v):
    return 0.5 * v * (1.0 + np.tanh(np.sqrt(2.0 / np.pi) * (v + 0.044715 * v**3)))


K, H, T, S, T2, P = 1536, 512, 4096, 1024, 2048, 1024


def setup_inputs():
    n = np.random.standard_normal
    s = mx_kscale(K)[:, None]
    u = mx_kscale(H)[:, None]
    d = {}
    d["tab_words"], d["tab_scales"] = pack_weight(n((K, T)) * s, "e4m3")
    d["offs"] = striped(np.random.permutation(T)[:S])
    d["offs2"] = striped(np.random.permutation(T2)[:S])
    d["offs3"] = striped(np.random.permutation(T2)[:P])
    d["offs4"] = striped(np.random.permutation(T2)[:P])
    d["w1"] = (n((K, H)) / K**0.5 / s).astype(np.float32)
    d["gain"] = (np.exp(0.3 * n(H)) * u[:, 0]).astype(np.float32)
    d["wgs"] = np.exp(0.3 * n((128, S))).astype(np.float32)
    d["page0"] = (n((H, T2)) * u).astype(np.float32)
    d["miss"] = np.exp(0.4 * n(H)).astype(np.float32)
    d["wp_words"], d["wp_scales"] = pack_weight(1.3 * n((H, H)) / H**0.5 / u, "e2m1")
    d["wn"] = (1.3 * n((H, H)) / H**0.5 / u).astype(np.float32)
    d["model"] = (0.7 * np.exp(0.3 * n(H)) / u[:, 0]).astype(np.float32)
    return d


def reference(tab_words, tab_scales, offs, offs2, offs3, offs4, w1, gain, wgs, page0, miss, wp_words, wp_scales, wn, model):
    v = unpack_weight(tab_words, tab_scales, "e4m3")[:, unstriped(offs)]
    h = f64(gain)[:, None] * (mxq(f64(w1), 0, "e4m3").T @ v)
    page = f64(page0).copy()
    page[:, unstriped(offs2)] = np.tile(f64(wgs), (H // 128, 1)) * h
    x = f64(miss)[:, None] * page[:, unstriped(offs3)]
    xp = mxq(np.maximum(x, 0.0), 0, "e4m3")
    xn = mxq(np.minimum(x, 0.0), 0, "e4m3")
    yp = unpack_weight(wp_words, wp_scales, "e2m1").T @ xp
    yn = mxq(f64(wn), 0, "e4m3").T @ xn
    y = np.maximum(yp, yn)
    out = y + f64(model)[:, None] * page[:, unstriped(offs4)]
    return out

@@ -1,0 +1,289 @@
+from contextlib import ExitStack
+
+import concourse.mybir as mybir
+
+K, H, T, S, T2, M = 1536, 512, 4096, 1024, 2048, 1024
+FLOPS = 2 * K * H * S + 2 * 2 * H * H * M
+
+F32 = mybir.dt.float32
+BF16 = mybir.dt.bfloat16
+I32 = mybir.dt.int32
+U32 = mybir.dt.uint32
+U16 = mybir.dt.uint16
+U8 = mybir.dt.uint8
+FP8X4 = mybir.dt.float8_e4m3fn_x4
+FP4X4 = mybir.dt.float4_e2m1fn_x4
+ALU = mybir.AluOpType
+ACT = mybir.ActivationFunctionType
+
+P = 128
+PACK = 4
+PASSES = K // (P * PACK)
+N = 512
+HALVES = S // N
+QUAD = 32
+LIST_COLS = N // 16
+
+
+def tile_list_stroke_page_coaching_kernel(
+    tc, tab_words, tab_scales, offs, offs2, offs3, offs4, w1, gain, wgs, page0, miss,
+    wp_words, wp_scales, wn, model, out,
+):
+    nc = tc.nc
+    with ExitStack() as ctx:
+        lists = ctx.enter_context(tc.tile_pool(name="lists", bufs=1))
+        keep = ctx.enter_context(tc.tile_pool(name="keep", bufs=1))
+        ring = ctx.enter_context(tc.tile_pool(name="ring", bufs=3))
+        psum = ctx.enter_context(tc.psum_pool(name="psum", bufs=8))
+
+        def cols(u):
+            return slice(u * N, (u + 1) * N)
+
+        def part(lst, u):
+            return lst[:, u * LIST_COLS : (u + 1) * LIST_COLS]
+
+        idx1 = lists.tile([P, S // 16], U16, name="idx1")
+        idx2 = lists.tile([P, S // 16], U16, name="idx2")
+        idx3 = lists.tile([P, M // 16], U16, name="idx3")
+        idx4 = lists.tile([P, M // 16], U16, name="idx4")
+
+        tab_sc = keep.tile([P, T], U8, name="tab_sc", align_bytes=64)
+        wp_sc_raw = keep.tile([P, H], U8, name="wp_sc_raw", align_bytes=64)
+        wp_raw = keep.tile([P, 2 * H], U8, name="wp_raw", align_bytes=64)
+        gain_sb = keep.tile([P, PACK], F32, name="gain_sb")
+        miss_sb = keep.tile([P, PACK], F32, name="miss_sb")
+        neg_miss = keep.tile([P, PACK], F32, name="neg_miss")
+        model_sb = keep.tile([P, PACK], F32, name="model_sb")
+
+        nc.vector.memset(tab_sc[:].bitcast(I32), 0)
+        nc.vector.memset(wp_sc_raw[:].bitcast(I32), 0)
+        for q in range(4):
+            nc.gpsimd.dma_start(
+                out=tab_sc[QUAD * q : QUAD * q + 4 * PASSES, :].bitcast(I32),
+                in_=tab_scales[:, 4 * q : 4 * q + 4, :].bitcast(I32),
+            )
+        nc.gpsimd.dma_start(out=gain_sb[:], in_=gain.rearrange("(p t) -> p t", t=PACK))
+        nc.gpsimd.dma_start(out=wp_raw[:].bitcast(I32), in_=wp_words[0].bitcast(I32))
+        for q in range(4):
+            nc.gpsimd.dma_start(
+                out=wp_sc_raw[QUAD * q : QUAD * q + 4, :].bitcast(I32),
+                in_=wp_scales[0, 4 * q : 4 * q + 4, :].bitcast(I32),
+            )
+        nc.gpsimd.dma_start(out=miss_sb[:], in_=miss.rearrange("(p t) -> p t", t=PACK))
+        nc.gpsimd.dma_start(out=model_sb[:], in_=model.rearrange("(p t) -> p t", t=PACK))
+
+        nc.sync.dma_start(idx1[:], offs)
+        tabs, w1_raw = [], []
+        for a in range(PASSES):
+            tab = ring.tile([P, T], I32, name="tab", tag="big")
+            nc.sync.dma_start(out=tab[:], in_=tab_words[a].rearrange("p t i -> p (t i)").bitcast(I32))
+            tabs.append(tab)
+            raw = ring.tile([P, PACK, H], F32, name="raw", tag="raw")
+            rows = w1[a * P * PACK : (a + 1) * P * PACK, :]
+            nc.sync.dma_start(out=raw[:], in_=rows.rearrange("(p j) c -> p j c", j=PACK))
+            w1_raw.append(raw)
+        nc.sync.dma_start(idx2[:], offs2)
+
+        pages = [keep.tile([P, T2], F32, name=f"page{t}") for t in range(PACK)]
+        page_rows = page0.rearrange("(p t) c -> p t c", t=PACK)
+        wgs_rows = wgs.rearrange("(q t) s -> q t s", t=PACK)
+        wgs_first = keep.tile([P, S], F32, name="wgs_first")
+        wgs_rest = keep.tile([P, (PACK - 1) * S], F32, name="wgs_rest")
+        nc.sync.dma_start(out=pages[0][:], in_=page_rows[:, 0, :])
+        for q in range(4):
+            nc.sync.dma_start(out=wgs_first[QUAD * q : QUAD * (q + 1), :], in_=wgs_rows[:, 0, :])
+        nc.sync.dma_start(idx3[:], offs3)
+        nc.sync.dma_start(out=pages[1][:], in_=page_rows[:, 1, :])
+        for q in range(4):
+            nc.sync.dma_start(
+                out=wgs_rest[QUAD * q : QUAD * (q + 1), :],
+                in_=wgs_rows[:, 1:, :].rearrange("q t s -> q (t s)"),
+            )
+        nc.sync.dma_start(out=pages[2][:], in_=page_rows[:, 2, :])
+        nc.sync.dma_start(idx4[:], offs4)
+        nc.sync.dma_start(out=pages[3][:], in_=page_rows[:, 3, :])
+        wn_raw = ring.tile([P, PACK, H], F32, name="wn_raw", tag="raw")
+        nc.sync.dma_start(out=wn_raw[:], in_=wn.rearrange("(p j) c -> p j c", j=PACK))
+
+        def wgs_of(t):
+            return wgs_first[:] if t == 0 else wgs_rest[:, (t - 1) * S : t * S]
+
+        def dealt(raw):
+            return raw[:].rearrange("p j (m t) -> p m t j", t=PACK)
+
+        def quantize(grouped, width, name):
+            codes = keep.tile([P, width], U32, name=name + "_codes", align_bytes=64)
+            scales = keep.tile([P, width], U8, name=name + "_scales", align_bytes=64)
+            nc.vector.quantize_mx(out=codes[:].bitcast(FP8X4), scales=scales[:], in_=grouped)
+            return codes, scales
+
+        def cast_whole(raw):
+            grouped = ring.tile([P, H * PACK], BF16, name="grouped", tag="grouped", align_bytes=64)
+            nc.scalar.copy(out=grouped[:].rearrange("p (t m j) -> p m t j", t=PACK, j=PACK), in_=dealt(raw))
+            return grouped
+
+        v_codes = []
+        v_scales = keep.tile([P, S], U8, name="v_scales", align_bytes=64)
+        w1_q = {}
+        for a in range(PASSES):
+            picked = ring.tile([P, S], U32, name="picked", tag="picked", align_bytes=64)
+            nc.vector.tensor_copy(picked[:], tabs[a][:].bitcast(U32).indirect(idx1[:]))
+            v_codes.append(picked)
+            if a == 0:
+                nc.vector.tensor_copy(v_scales[:], tab_sc[:].indirect(idx1[:]))
+            if a < PASSES - 1:
+                codes, scales = quantize(cast_whole(w1_raw[a])[:], H, f"w1_{a}")
+                for t in range(PACK):
+                    w1_q[a, t] = (codes[:, t * P : (t + 1) * P], scales[:, t * P : (t + 1) * P])
+            if a == 1:
+                wp_codes = keep.tile([P, 2 * H], U8, name="wp_codes", align_bytes=64)
+                wp_sc = keep.tile([P, H], U8, name="wp_sc", align_bytes=64)
+                nc.vector.tensor_copy(
+                    out=wp_codes[:].rearrange("p (t m b) -> p m t b", t=PACK, b=2),
+                    in_=wp_raw[:].rearrange("p (m t b) -> p m t b", t=PACK, b=2),
+                )
+                nc.vector.tensor_copy(
+                    out=wp_sc[:].rearrange("p (t m) -> p m t", t=PACK),
+                    in_=wp_sc_raw[:].rearrange("p (m t) -> p m t", t=PACK),
+                )
+                nc.vector.tensor_scalar(neg_miss[:], miss_sb[:], -1.0, None, ALU.mult)
+
+        last = PASSES - 1
+        first_bf = keep.tile([P, P * PACK], BF16, name="first_bf", align_bytes=64)
+        rest_bf = ring.tile([P, (PACK - 1) * P * PACK], BF16, name="rest_bf", tag="grouped", align_bytes=64)
+        nc.vector.tensor_copy(
+            out=first_bf[:].rearrange("p (m j) -> p m j", j=PACK), in_=dealt(w1_raw[last])[:, :, 0, :]
+        )
+        nc.scalar.copy(
+            out=rest_bf[:].rearrange("p (t m j) -> p m t j", t=PACK - 1, j=PACK),
+            in_=dealt(w1_raw[last])[:, :, 1:, :],
+        )
+        codes, scales = quantize(first_bf[:], P, "w1_last0")
+        w1_q[last, 0] = (codes[:], scales[:])
+
+        def product_h(t, u):
+            acc = psum.tile([P, N], F32, name="acc", tag="acc")
+            for a in range(PASSES):
+                nc.tensor.matmul_mx(
+                    out=acc[:],
+                    lhsT=w1_q[a, t][0].bitcast(FP8X4),
+                    lhsT_scale=w1_q[a, t][1],
+                    rhs=v_codes[a][:, cols(u)].bitcast(FP8X4),
+                    rhs_scale=v_scales[4 * a :, cols(u)],
+                    start=(a == 0),
+                    stop=(a == last),
+                )
+            return acc
+
+        def scatter(t, offsets, values, weights):
+            nc.vector.tensor_tensor(pages[t][:].indirect(offsets), values, weights, ALU.mult)
+
+        h_first = [keep.tile([P, N], F32, name=f"h_first{u}") for u in range(HALVES)]
+        nc.vector.tensor_scalar(h_first[0][:], product_h(0, 0)[:], gain_sb[:, 0:1], None, ALU.mult)
+        nc.scalar.activation(h_first[1][:], product_h(0, 1)[:], ACT.Copy, scale=gain_sb[:, 0:1])
+        scatter(0, part(idx2, 0), h_first[0][:], wgs_first[:, cols(0)])
+        for t in range(1, PACK):
+            codes, scales = quantize(rest_bf[:, (t - 1) * N : t * N], P, f"w1_last{t}")
+            w1_q[last, t] = (codes[:], scales[:])
+        scatter(0, part(idx2, 1), h_first[1][:], wgs_first[:, cols(1)])
+
+        h = {}
+        for t in range(1, PACK):
+            h[t] = keep.tile([P, S], F32, name=f"h{t}", tag=f"h{t}")
+            for u in range(HALVES):
+                nc.scalar.activation(h[t][:, cols(u)], product_h(t, u)[:], ACT.Copy, scale=gain_sb[:, t : t + 1])
+
+        x_low = ring.tile([P, 2, M], F32, name="x_low", tag="raw")
+        x_high = [keep.tile([P, 2, N], F32, name=f"x_high{u}") for u in range(HALVES)]
+        xp_bf = [keep.tile([P, N, PACK], BF16, name=f"xp_bf{u}", align_bytes=64) for u in range(HALVES)]
+        xn_bf = [keep.tile([P, N, PACK], BF16, name=f"xn_bf{u}", align_bytes=64) for u in range(HALVES)]
+
+        def signed_parts(u, t, source):
+            nc.scalar.activation(xp_bf[u][:, :, t], source, ACT.Relu, scale=miss_sb[:, t : t + 1])
+            nc.scalar.activation(xn_bf[u][:, :, t], source, ACT.Relu, scale=neg_miss[:, t : t + 1])
+
+        def gather_missed(t):
+            if t < 2:
+                nc.vector.tensor_copy(x_low[:, t, :], pages[t][:].indirect(idx3[:]))
+            else:
+                for u in range(HALVES):
+                    nc.vector.tensor_copy(x_high[u][:, t - 2, :], pages[t][:].indirect(part(idx3, u)))
+            for u in range(HALVES):
+                signed_parts(u, t, x_low[:, t, cols(u)] if t < 2 else x_high[u][:, t - 2, :])
+
+        strokes = {}
+
+        def gather_model(t):
+            if t == 2:
+                strokes[t] = keep.tile([P, M], F32, name="strokes2", tag="h3")
+            else:
+                strokes[t] = ring.tile([P, M], F32, name="strokes", tag="big")
+            nc.vector.tensor_copy(strokes[t][:], pages[t][:].indirect(idx4[:]))
+
+        scatter(1, idx2[:], h[1][:], wgs_of(1))
+        gather_missed(0)
+        scatter(2, idx2[:], h[2][:], wgs_of(2))
+        gather_missed(1)
+        wn_codes, wn_scales = quantize(cast_whole(wn_raw)[:], H, "wn")
+        gather_model(0)
+        gather_missed(2)
+        gather_model(1)
+        scatter(3, idx2[:], h[3][:], wgs_of(3))
+        gather_missed(3)
+        gather_model(3)
+        xq = []
+        for u in range(HALVES):
+            xq.append(
+                (
+                    quantize(xp_bf[u][:].rearrange("p m j -> p (m j)"), N, f"xp{u}"),
+                    quantize(xn_bf[u][:].rearrange("p m j -> p (m j)"), N, f"xn{u}"),
+                )
+            )
+            if u == 0:
+                gather_model(2)
+
+        out_rows = out.rearrange("(p t) m -> p t m", t=PACK)
+
+        def larger(t, u):
+            (xp_c, xp_s), (xn_c, xn_s) = xq[u]
+            yn = psum.tile([P, N], F32, name="yn", tag="acc")
+            nc.tensor.matmul_mx(
+                out=yn[:],
+                lhsT=wn_codes[:, t * P : (t + 1) * P].bitcast(FP8X4),
+                lhsT_scale=wn_scales[:, t * P : (t + 1) * P],
+                rhs=xn_c[:].bitcast(FP8X4),
+                rhs_scale=xn_s[:],
+                start=True,
+                stop=True,
+            )
+            yp = psum.tile([P, N], F32, name="yp", tag="acc")
+            nc.tensor.matmul_mx(
+                out=yp[:],
+                lhsT=wp_codes[:, 2 * t * P : 2 * (t + 1) * P].bitcast(FP4X4),
+                lhsT_scale=wp_sc[:, t * P : (t + 1) * P],
+                rhs=xp_c[:].bitcast(FP8X4),
+                rhs_scale=xp_s[:],
+                start=True,
+                stop=True,
+            )
+            yn_sb = ring.tile([P, N], F32, name="yn_sb", tag="picked", align_bytes=64)
+            nc.scalar.activation(yn_sb[:], yn[:], ACT.Copy, scale=-1.0)
+            y = ring.tile([P, N], F32, name="y", tag="y")
+            nc.vector.tensor_tensor(y[:], yp[:], yn_sb[:], ALU.max)
+            return y
+
+        def finish(t, u, y):
+            res = ring.tile([P, N], F32, name="res", tag="res")
+            nc.vector.scalar_tensor_tensor(
+                res[:], strokes[t][:, cols(u)], model_sb[:, t : t + 1], y[:], ALU.mult, ALU.add
+            )
+            nc.sync.dma_start(out=out_rows[:, t, cols(u)], in_=res[:])
+
+        steps = [(t, u) for u in range(HALVES) for t in range(PACK)]
+        waiting = None
+        for t, u in steps:
+            y = larger(t, u)
+            if waiting is not None:
+                finish(*waiting)
+            waiting = (t, u, y)
+        finish(*waiting)

@@ -57,31 +57,42 @@ def tile_list_stroke_page_coaching_kernel(
 
         nc.vector.memset(tab_sc[:].bitcast(I32), 0)
         nc.vector.memset(wp_sc_raw[:].bitcast(I32), 0)
+
+        def load_tab(a):
+            tab = ring.tile([P, T], I32, name="tab", tag="big")
+            nc.sync.dma_start(out=tab[:], in_=tab_words[a].rearrange("p t i -> p (t i)").bitcast(I32))
+            return tab
+
+        def load_rows(rows):
+            raw = ring.tile([P, PACK, H], F32, name="raw", tag="raw")
+            nc.sync.dma_start(out=raw[:], in_=rows.rearrange("(p j) c -> p j c", j=PACK))
+            return raw
+
+        def load_w1(a):
+            return load_rows(w1[a * P * PACK : (a + 1) * P * PACK, :])
+
+        def load_vector(tile, vec):
+            nc.sync.dma_start(out=tile[:], in_=vec.rearrange("(p t) -> p t", t=PACK))
+
+        nc.sync.dma_start(idx1[:], offs)
+        tabs = [load_tab(0)]
         for q in range(4):
-            nc.gpsimd.dma_start(
+            nc.sync.dma_start(
                 out=tab_sc[QUAD * q : QUAD * q + 4 * PASSES, :].bitcast(I32),
                 in_=tab_scales[:, 4 * q : 4 * q + 4, :].bitcast(I32),
             )
-        nc.gpsimd.dma_start(out=gain_sb[:], in_=gain.rearrange("(p t) -> p t", t=PACK))
-        nc.gpsimd.dma_start(out=wp_raw[:].bitcast(I32), in_=wp_words[0].bitcast(I32))
+        w1_raw = [load_w1(0)]
+        tabs.append(load_tab(1))
+        nc.sync.dma_start(out=wp_raw[:].bitcast(I32), in_=wp_words[0].bitcast(I32))
         for q in range(4):
-            nc.gpsimd.dma_start(
+            nc.sync.dma_start(
                 out=wp_sc_raw[QUAD * q : QUAD * q + 4, :].bitcast(I32),
                 in_=wp_scales[0, 4 * q : 4 * q + 4, :].bitcast(I32),
             )
-        nc.gpsimd.dma_start(out=miss_sb[:], in_=miss.rearrange("(p t) -> p t", t=PACK))
-        nc.gpsimd.dma_start(out=model_sb[:], in_=model.rearrange("(p t) -> p t", t=PACK))
-
-        nc.sync.dma_start(idx1[:], offs)
-        tabs, w1_raw = [], []
-        for a in range(PASSES):
-            tab = ring.tile([P, T], I32, name="tab", tag="big")
-            nc.sync.dma_start(out=tab[:], in_=tab_words[a].rearrange("p t i -> p (t i)").bitcast(I32))
-            tabs.append(tab)
-            raw = ring.tile([P, PACK, H], F32, name="raw", tag="raw")
-            rows = w1[a * P * PACK : (a + 1) * P * PACK, :]
-            nc.sync.dma_start(out=raw[:], in_=rows.rearrange("(p j) c -> p j c", j=PACK))
-            w1_raw.append(raw)
+        w1_raw.append(load_w1(1))
+        tabs.append(load_tab(2))
+        load_vector(gain_sb, gain)
+        w1_raw.append(load_w1(2))
         nc.sync.dma_start(idx2[:], offs2)
 
         pages = [keep.tile([P, T2], F32, name=f"page{t}") for t in range(PACK)]
@@ -92,6 +103,7 @@ def tile_list_stroke_page_coaching_kernel(
         nc.sync.dma_start(out=pages[0][:], in_=page_rows[:, 0, :])
         for q in range(4):
             nc.sync.dma_start(out=wgs_first[QUAD * q : QUAD * (q + 1), :], in_=wgs_rows[:, 0, :])
+        load_vector(miss_sb, miss)
         nc.sync.dma_start(idx3[:], offs3)
         nc.sync.dma_start(out=pages[1][:], in_=page_rows[:, 1, :])
         for q in range(4):
@@ -99,11 +111,11 @@ def tile_list_stroke_page_coaching_kernel(
                 out=wgs_rest[QUAD * q : QUAD * (q + 1), :],
                 in_=wgs_rows[:, 1:, :].rearrange("q t s -> q (t s)"),
             )
+        wn_raw = load_rows(wn)
         nc.sync.dma_start(out=pages[2][:], in_=page_rows[:, 2, :])
         nc.sync.dma_start(idx4[:], offs4)
         nc.sync.dma_start(out=pages[3][:], in_=page_rows[:, 3, :])
-        wn_raw = ring.tile([P, PACK, H], F32, name="wn_raw", tag="raw")
-        nc.sync.dma_start(out=wn_raw[:], in_=wn.rearrange("(p j) c -> p j c", j=PACK))
+        load_vector(model_sb, model)
 
         def wgs_of(t):
             return wgs_first[:] if t == 0 else wgs_rest[:, (t - 1) * S : t * S]
@@ -146,7 +158,6 @@ def tile_list_stroke_page_coaching_kernel(
                     out=wp_sc[:].rearrange("p (t m) -> p m t", t=PACK),
                     in_=wp_sc_raw[:].rearrange("p (m t) -> p m t", t=PACK),
                 )
-                nc.vector.tensor_scalar(neg_miss[:], miss_sb[:], -1.0, None, ALU.mult)
 
         last = PASSES - 1
         first_bf = keep.tile([P, P * PACK], BF16, name="first_bf", align_bytes=64)
@@ -193,10 +204,12 @@ def tile_list_stroke_page_coaching_kernel(
             for u in range(HALVES):
                 nc.scalar.activation(h[t][:, cols(u)], product_h(t, u)[:], ACT.Copy, scale=gain_sb[:, t : t + 1])
 
-        x_low = ring.tile([P, 2, M], F32, name="x_low", tag="raw")
+        x_low = keep.tile([P, 2, M], F32, name="x_low")
         x_high = [keep.tile([P, 2, N], F32, name=f"x_high{u}") for u in range(HALVES)]
         xp_bf = [keep.tile([P, N, PACK], BF16, name=f"xp_bf{u}", align_bytes=64) for u in range(HALVES)]
-        xn_bf = [keep.tile([P, N, PACK], BF16, name=f"xn_bf{u}", align_bytes=64) for u in range(HALVES)]
+        xn_bf = [keep.tile([P, N, PACK], BF16, name=f"xn_bf{u}", tag=f"xn_bf{u}", align_bytes=64) for u in range(HALVES)]
+
+        nc.scalar.activation(neg_miss[:], miss_sb[:], ACT.Copy, scale=-1.0)
 
         def signed_parts(u, t, source):
             nc.scalar.activation(xp_bf[u][:, :, t], source, ACT.Relu, scale=miss_sb[:, t : t + 1])
@@ -215,7 +228,7 @@ def tile_list_stroke_page_coaching_kernel(
 
         def gather_model(t):
             if t == 2:
-                strokes[t] = keep.tile([P, M], F32, name="strokes2", tag="h3")
+                strokes[t] = keep.tile([P, M], F32, name="strokes2", tag="xn_bf0", align_bytes=64)
             else:
                 strokes[t] = ring.tile([P, M], F32, name="strokes", tag="big")
             nc.vector.tensor_copy(strokes[t][:], pages[t][:].indirect(idx4[:]))

@@ -52,7 +52,6 @@ def tile_list_stroke_page_coaching_kernel(
         wp_raw = keep.tile([P, 2 * H], U8, name="wp_raw", align_bytes=64)
         gain_sb = keep.tile([P, PACK], F32, name="gain_sb")
         miss_sb = keep.tile([P, PACK], F32, name="miss_sb")
-        neg_miss = keep.tile([P, PACK], F32, name="neg_miss")
         model_sb = keep.tile([P, PACK], F32, name="model_sb")
 
         nc.vector.memset(tab_sc[:].bitcast(I32), 0)
@@ -200,60 +199,52 @@ def tile_list_stroke_page_coaching_kernel(
 
         h = {}
         for t in range(1, PACK):
-            h[t] = keep.tile([P, S], F32, name=f"h{t}", tag=f"h{t}")
+            h[t] = keep.tile([P, S], F32, name=f"h{t}", tag=f"h{t}", align_bytes=64)
             for u in range(HALVES):
                 nc.scalar.activation(h[t][:, cols(u)], product_h(t, u)[:], ACT.Copy, scale=gain_sb[:, t : t + 1])
 
-        x_low = keep.tile([P, 2, M], F32, name="x_low")
-        x_high = [keep.tile([P, 2, N], F32, name=f"x_high{u}") for u in range(HALVES)]
-        xp_bf = [keep.tile([P, N, PACK], BF16, name=f"xp_bf{u}", align_bytes=64) for u in range(HALVES)]
-        xn_bf = [keep.tile([P, N, PACK], BF16, name=f"xn_bf{u}", tag=f"xn_bf{u}", align_bytes=64) for u in range(HALVES)]
+        x = [keep.tile([P, PACK, N], F32, name=f"x{u}") for u in range(HALVES)]
 
-        nc.scalar.activation(neg_miss[:], miss_sb[:], ACT.Copy, scale=-1.0)
-
-        def signed_parts(u, t, source):
-            nc.scalar.activation(xp_bf[u][:, :, t], source, ACT.Relu, scale=miss_sb[:, t : t + 1])
-            nc.scalar.activation(xn_bf[u][:, :, t], source, ACT.Relu, scale=neg_miss[:, t : t + 1])
+        def scale_missed(t, u, source):
+            nc.scalar.activation(x[u][:, t, :], source, ACT.Copy, scale=miss_sb[:, t : t + 1])
 
         def gather_missed(t):
-            if t < 2:
-                nc.vector.tensor_copy(x_low[:, t, :], pages[t][:].indirect(idx3[:]))
-            else:
-                for u in range(HALVES):
-                    nc.vector.tensor_copy(x_high[u][:, t - 2, :], pages[t][:].indirect(part(idx3, u)))
+            missed = ring.tile([P, M], F32, name="missed", tag="big")
+            nc.vector.tensor_copy(missed[:], pages[t][:].indirect(idx3[:]))
             for u in range(HALVES):
-                signed_parts(u, t, x_low[:, t, cols(u)] if t < 2 else x_high[u][:, t - 2, :])
+                scale_missed(t, u, missed[:, cols(u)])
+
+        def gather_missed_half(t, u):
+            missed = ring.tile([P, N], F32, name="missed_half", tag="big")
+            nc.vector.tensor_copy(missed[:], pages[t][:].indirect(part(idx3, u)))
+            return missed
+
+        def signed_part(u, sign, name):
+            grouped = keep.tile([P, N * PACK], BF16, name=name, tag=name, align_bytes=64)
+            nc.scalar.activation(
+                grouped[:].rearrange("p (c i t) -> p c t i", i=4, t=PACK),
+                x[u][:].rearrange("p t (c i) -> p c t i", i=4),
+                ACT.Relu,
+                scale=sign,
+            )
+            return quantize(grouped[:], N, name)
 
         strokes = {}
 
-        def gather_model(t):
-            if t == 2:
-                strokes[t] = keep.tile([P, M], F32, name="strokes2", tag="xn_bf0", align_bytes=64)
-            else:
-                strokes[t] = ring.tile([P, M], F32, name="strokes", tag="big")
-            nc.vector.tensor_copy(strokes[t][:], pages[t][:].indirect(idx4[:]))
+        def gather_model(ts, u, tag):
+            pair = keep.tile([P, M], F32, name="strokes_" + tag, tag=tag, align_bytes=64)
+            for i, t in enumerate(ts):
+                nc.vector.tensor_copy(pair[:, cols(i)], pages[t][:].indirect(part(idx4, u)))
+                strokes[t, u] = pair[:, cols(i)]
 
         scatter(1, idx2[:], h[1][:], wgs_of(1))
         gather_missed(0)
         scatter(2, idx2[:], h[2][:], wgs_of(2))
         gather_missed(1)
         wn_codes, wn_scales = quantize(cast_whole(wn_raw)[:], H, "wn")
-        gather_model(0)
         gather_missed(2)
-        gather_model(1)
         scatter(3, idx2[:], h[3][:], wgs_of(3))
-        gather_missed(3)
-        gather_model(3)
-        xq = []
-        for u in range(HALVES):
-            xq.append(
-                (
-                    quantize(xp_bf[u][:].rearrange("p m j -> p (m j)"), N, f"xp{u}"),
-                    quantize(xn_bf[u][:].rearrange("p m j -> p (m j)"), N, f"xn{u}"),
-                )
-            )
-            if u == 0:
-                gather_model(2)
+        missed_last = [gather_missed_half(3, u) for u in range(HALVES)]
 
         out_rows = out.rearrange("(p t) m -> p t m", t=PACK)
 
@@ -288,15 +279,29 @@ def tile_list_stroke_page_coaching_kernel(
         def finish(t, u, y):
             res = ring.tile([P, N], F32, name="res", tag="res")
             nc.vector.scalar_tensor_tensor(
-                res[:], strokes[t][:, cols(u)], model_sb[:, t : t + 1], y[:], ALU.mult, ALU.add
+                res[:], strokes[t, u], model_sb[:, t : t + 1], y[:], ALU.mult, ALU.add
             )
             nc.sync.dma_start(out=out_rows[:, t, cols(u)], in_=res[:])
 
-        steps = [(t, u) for u in range(HALVES) for t in range(PACK)]
-        waiting = None
-        for t, u in steps:
-            y = larger(t, u)
-            if waiting is not None:
-                finish(*waiting)
-            waiting = (t, u, y)
-        finish(*waiting)
+        def results(u):
+            waiting = None
+            for t in range(PACK):
+                y = larger(t, u)
+                if waiting is not None:
+                    finish(*waiting)
+                waiting = (t, u, y)
+            finish(*waiting)
+
+        xq = {}
+        scale_missed(3, 0, missed_last[0][:])
+        gather_model((0, 1), 0, "h3")
+        xp = signed_part(0, 1.0, "xp0")
+        gather_model((2, 3), 0, "xp0")
+        xq[0] = (xp, signed_part(0, -1.0, "xn0"))
+        gather_model((0, 1), 1, "xn0")
+        scale_missed(3, 1, missed_last[1][:])
+        xp = signed_part(1, 1.0, "xp1")
+        results(0)
+        xq[1] = (xp, signed_part(1, -1.0, "xn1"))
+        gather_model((2, 3), 1, "xn1")
+        results(1)

@@ -19,6 +19,7 @@ ACT = mybir.ActivationFunctionType
 P = 128
 PACK = 4
 PASSES = K // (P * PACK)
+BLOCKS = H // P
 N = 512
 HALVES = S // N
 QUAD = 32
@@ -39,6 +40,9 @@ def tile_list_stroke_page_coaching_kernel(
         def cols(u):
             return slice(u * N, (u + 1) * N)
 
+        def rows(b):
+            return slice(b * P, (b + 1) * P)
+
         def part(lst, u):
             return lst[:, u * LIST_COLS : (u + 1) * LIST_COLS]
 
@@ -48,31 +52,44 @@ def tile_list_stroke_page_coaching_kernel(
         idx4 = lists.tile([P, M // 16], U16, name="idx4")
 
         tab_sc = keep.tile([P, T], U8, name="tab_sc", align_bytes=64)
-        wp_sc_raw = keep.tile([P, H], U8, name="wp_sc_raw", align_bytes=64)
-        wp_raw = keep.tile([P, 2 * H], U8, name="wp_raw", align_bytes=64)
-        gain_sb = keep.tile([P, PACK], F32, name="gain_sb")
-        miss_sb = keep.tile([P, PACK], F32, name="miss_sb")
-        model_sb = keep.tile([P, PACK], F32, name="model_sb")
+        wp_sc = keep.tile([P, H], U8, name="wp_sc", align_bytes=64)
+        wp_codes = keep.tile([P, 2 * H], U8, name="wp_codes", align_bytes=64)
+        gains = [keep.tile([P, 1], F32, name=f"gain{b}", tag=f"gain{b}") for b in range(BLOCKS)]
+        miss_sb = keep.tile([P, BLOCKS], F32, name="miss_sb")
+        model_sb = keep.tile([P, BLOCKS], F32, name="model_sb")
+        pages = [keep.tile([P, T2], F32, name=f"page{b}") for b in range(BLOCKS)]
+        wgs_sb = keep.tile([P, S], F32, name="wgs_sb")
 
         nc.vector.memset(tab_sc[:].bitcast(I32), 0)
-        nc.vector.memset(wp_sc_raw[:].bitcast(I32), 0)
+        nc.vector.memset(wp_sc[:].bitcast(I32), 0)
 
         def load_tab(a):
-            tab = ring.tile([P, T], I32, name="tab", tag="big")
+            tab = keep.tile([P, T], I32, name=f"tab{a}", tag=f"tab{a}", align_bytes=64)
             nc.sync.dma_start(out=tab[:], in_=tab_words[a].rearrange("p t i -> p (t i)").bitcast(I32))
             return tab
 
-        def load_rows(rows):
-            raw = ring.tile([P, PACK, H], F32, name="raw", tag="raw")
-            nc.sync.dma_start(out=raw[:], in_=rows.rearrange("(p j) c -> p j c", j=PACK))
+        def load_weight(weight, tag):
+            raw = keep.tile([P, PACK, weight.shape[1]], F32, name="raw_" + tag, tag=tag, align_bytes=64)
+            nc.sync.dma_start(out=raw[:], in_=weight.rearrange("(p j) c -> p j c", j=PACK))
             return raw
 
-        def load_w1(a):
-            return load_rows(w1[a * P * PACK : (a + 1) * P * PACK, :])
+        def load_w1(a, b0, b1):
+            raw = load_weight(w1[a * P * PACK : (a + 1) * P * PACK, b0 * P : b1 * P], f"w1_raw{a}_{b0}")
+            for b in range(b0, b1):
+                w1_raw[a, b] = raw[:, :, rows(b - b0)]
 
         def load_vector(tile, vec):
-            nc.sync.dma_start(out=tile[:], in_=vec.rearrange("(p t) -> p t", t=PACK))
+            with nc.allow_non_contiguous_dma(reason="one value of a row vector to each partition"):
+                nc.sync.dma_start(out=tile[:], in_=vec.rearrange("(b p) -> p b", p=P))
 
+        def load_gain(b):
+            with nc.allow_non_contiguous_dma(reason="one value of a row vector to each partition"):
+                nc.sync.dma_start(out=gains[b][:], in_=gain[rows(b)].rearrange("(p o) -> p o", o=1))
+
+        def load_page(b):
+            nc.sync.dma_start(out=pages[b][:], in_=page0[rows(b), :])
+
+        w1_raw = {}
         nc.sync.dma_start(idx1[:], offs)
         tabs = [load_tab(0)]
         for q in range(4):
@@ -80,181 +97,157 @@ def tile_list_stroke_page_coaching_kernel(
                 out=tab_sc[QUAD * q : QUAD * q + 4 * PASSES, :].bitcast(I32),
                 in_=tab_scales[:, 4 * q : 4 * q + 4, :].bitcast(I32),
             )
-        w1_raw = [load_w1(0)]
+        load_w1(0, 0, 1)
+        load_w1(1, 0, 1)
         tabs.append(load_tab(1))
-        nc.sync.dma_start(out=wp_raw[:].bitcast(I32), in_=wp_words[0].bitcast(I32))
-        for q in range(4):
-            nc.sync.dma_start(
-                out=wp_sc_raw[QUAD * q : QUAD * q + 4, :].bitcast(I32),
-                in_=wp_scales[0, 4 * q : 4 * q + 4, :].bitcast(I32),
-            )
-        w1_raw.append(load_w1(1))
-        tabs.append(load_tab(2))
-        load_vector(gain_sb, gain)
-        w1_raw.append(load_w1(2))
+        load_w1(2, 0, 1)
+        load_gain(0)
         nc.sync.dma_start(idx2[:], offs2)
-
-        pages = [keep.tile([P, T2], F32, name=f"page{t}") for t in range(PACK)]
-        page_rows = page0.rearrange("(p t) c -> p t c", t=PACK)
-        wgs_rows = wgs.rearrange("(q t) s -> q t s", t=PACK)
-        wgs_first = keep.tile([P, S], F32, name="wgs_first")
-        wgs_rest = keep.tile([P, (PACK - 1) * S], F32, name="wgs_rest")
-        nc.sync.dma_start(out=pages[0][:], in_=page_rows[:, 0, :])
-        for q in range(4):
-            nc.sync.dma_start(out=wgs_first[QUAD * q : QUAD * (q + 1), :], in_=wgs_rows[:, 0, :])
+        tabs.append(load_tab(2))
+        load_page(0)
+        for u in range(HALVES):
+            nc.sync.dma_start(out=wgs_sb[:, cols(u)], in_=wgs[:, cols(u)])
+        for a in range(PASSES):
+            load_w1(a, 1, 2)
+        load_gain(1)
         load_vector(miss_sb, miss)
         nc.sync.dma_start(idx3[:], offs3)
-        nc.sync.dma_start(out=pages[1][:], in_=page_rows[:, 1, :])
+        load_page(1)
+        for a in range(PASSES):
+            load_w1(a, 2, BLOCKS)
+        load_gain(2)
+        wn_raw = load_weight(wn, "tab1")
+        load_page(2)
+        load_gain(3)
+        load_page(3)
+        nc.sync.dma_start(idx4[:], offs4)
+        nc.sync.dma_start(out=wp_codes[:].bitcast(I32), in_=wp_words[0].bitcast(I32))
         for q in range(4):
             nc.sync.dma_start(
-                out=wgs_rest[QUAD * q : QUAD * (q + 1), :],
-                in_=wgs_rows[:, 1:, :].rearrange("q t s -> q (t s)"),
+                out=wp_sc[QUAD * q : QUAD * q + 4, :].bitcast(I32),
+                in_=wp_scales[0, 4 * q : 4 * q + 4, :].bitcast(I32),
             )
-        wn_raw = load_rows(wn)
-        nc.sync.dma_start(out=pages[2][:], in_=page_rows[:, 2, :])
-        nc.sync.dma_start(idx4[:], offs4)
-        nc.sync.dma_start(out=pages[3][:], in_=page_rows[:, 3, :])
         load_vector(model_sb, model)
 
-        def wgs_of(t):
-            return wgs_first[:] if t == 0 else wgs_rest[:, (t - 1) * S : t * S]
+        def interleave(grouped, source, func, scale):
+            nc.scalar.activation(
+                grouped.rearrange("p (c i j) -> p c j i", i=4, j=PACK),
+                source.rearrange("p j (c i) -> p c j i", i=4),
+                func,
+                scale=scale,
+            )
 
-        def dealt(raw):
-            return raw[:].rearrange("p j (m t) -> p m t j", t=PACK)
-
-        def quantize(grouped, width, name):
-            codes = keep.tile([P, width], U32, name=name + "_codes", align_bytes=64)
+        def quantize(grouped, width, name, codes_tag=None):
+            codes = keep.tile([P, width], U32, name=name + "_codes", tag=codes_tag or name + "_codes", align_bytes=64)
             scales = keep.tile([P, width], U8, name=name + "_scales", align_bytes=64)
             nc.vector.quantize_mx(out=codes[:].bitcast(FP8X4), scales=scales[:], in_=grouped)
             return codes, scales
 
-        def cast_whole(raw):
-            grouped = ring.tile([P, H * PACK], BF16, name="grouped", tag="grouped", align_bytes=64)
-            nc.scalar.copy(out=grouped[:].rearrange("p (t m j) -> p m t j", t=PACK, j=PACK), in_=dealt(raw))
-            return grouped
-
-        v_codes = []
-        v_scales = keep.tile([P, S], U8, name="v_scales", align_bytes=64)
         w1_q = {}
-        for a in range(PASSES):
-            picked = ring.tile([P, S], U32, name="picked", tag="picked", align_bytes=64)
+
+        def quantize_w1(b):
+            grouped = keep.tile([P, PASSES * P * PACK], BF16, name=f"w1_bf{b}", tag=f"w1_bf{b}", align_bytes=64)
+            for a in range(PASSES):
+                interleave(grouped[:, cols(a)], w1_raw[a, b], ACT.Copy, 1.0)
+            codes, scales = quantize(grouped[:, : 2 * N], 2 * P, f"w1_{b}_low")
+            for a in range(2):
+                w1_q[a, b] = (codes[:, rows(a)], scales[:, rows(a)])
+            codes, scales = quantize(grouped[:, 2 * N :], P, f"w1_{b}_high")
+            w1_q[2, b] = (codes[:], scales[:])
+
+        v_codes = {}
+        v_scales = keep.tile([P, S], U8, name="v_scales", align_bytes=64)
+        last = PASSES - 1
+        for a in range(last):
+            picked = keep.tile([P, S], U32, name=f"picked{a}", align_bytes=64)
             nc.vector.tensor_copy(picked[:], tabs[a][:].bitcast(U32).indirect(idx1[:]))
-            v_codes.append(picked)
+            for u in range(HALVES):
+                v_codes[a, u] = picked[:, cols(u)]
             if a == 0:
                 nc.vector.tensor_copy(v_scales[:], tab_sc[:].indirect(idx1[:]))
-            if a < PASSES - 1:
-                codes, scales = quantize(cast_whole(w1_raw[a])[:], H, f"w1_{a}")
-                for t in range(PACK):
-                    w1_q[a, t] = (codes[:, t * P : (t + 1) * P], scales[:, t * P : (t + 1) * P])
-            if a == 1:
-                wp_codes = keep.tile([P, 2 * H], U8, name="wp_codes", align_bytes=64)
-                wp_sc = keep.tile([P, H], U8, name="wp_sc", align_bytes=64)
-                nc.vector.tensor_copy(
-                    out=wp_codes[:].rearrange("p (t m b) -> p m t b", t=PACK, b=2),
-                    in_=wp_raw[:].rearrange("p (m t b) -> p m t b", t=PACK, b=2),
-                )
-                nc.vector.tensor_copy(
-                    out=wp_sc[:].rearrange("p (t m) -> p m t", t=PACK),
-                    in_=wp_sc_raw[:].rearrange("p (m t) -> p m t", t=PACK),
-                )
+                quantize_w1(0)
 
-        last = PASSES - 1
-        first_bf = keep.tile([P, P * PACK], BF16, name="first_bf", align_bytes=64)
-        rest_bf = ring.tile([P, (PACK - 1) * P * PACK], BF16, name="rest_bf", tag="grouped", align_bytes=64)
-        nc.vector.tensor_copy(
-            out=first_bf[:].rearrange("p (m j) -> p m j", j=PACK), in_=dealt(w1_raw[last])[:, :, 0, :]
-        )
-        nc.scalar.copy(
-            out=rest_bf[:].rearrange("p (t m j) -> p m t j", t=PACK - 1, j=PACK),
-            in_=dealt(w1_raw[last])[:, :, 1:, :],
-        )
-        codes, scales = quantize(first_bf[:], P, "w1_last0")
-        w1_q[last, 0] = (codes[:], scales[:])
+        def gather_last(u):
+            picked = keep.tile([P, N], U32, name=f"picked_last{u}", align_bytes=64)
+            nc.vector.tensor_copy(picked[:], tabs[last][:].bitcast(U32).indirect(part(idx1, u)))
+            v_codes[last, u] = picked[:]
 
-        def product_h(t, u):
+        def product_h(b, u):
             acc = psum.tile([P, N], F32, name="acc", tag="acc")
             for a in range(PASSES):
                 nc.tensor.matmul_mx(
                     out=acc[:],
-                    lhsT=w1_q[a, t][0].bitcast(FP8X4),
-                    lhsT_scale=w1_q[a, t][1],
-                    rhs=v_codes[a][:, cols(u)].bitcast(FP8X4),
+                    lhsT=w1_q[a, b][0].bitcast(FP8X4),
+                    lhsT_scale=w1_q[a, b][1],
+                    rhs=v_codes[a, u].bitcast(FP8X4),
                     rhs_scale=v_scales[4 * a :, cols(u)],
                     start=(a == 0),
                     stop=(a == last),
                 )
             return acc
 
-        def scatter(t, offsets, values, weights):
-            nc.vector.tensor_tensor(pages[t][:].indirect(offsets), values, weights, ALU.mult)
+        def features(b, u, h):
+            nc.scalar.activation(h, product_h(b, u)[:], ACT.Copy, scale=gains[b][:])
 
-        h_first = [keep.tile([P, N], F32, name=f"h_first{u}") for u in range(HALVES)]
-        nc.vector.tensor_scalar(h_first[0][:], product_h(0, 0)[:], gain_sb[:, 0:1], None, ALU.mult)
-        nc.scalar.activation(h_first[1][:], product_h(0, 1)[:], ACT.Copy, scale=gain_sb[:, 0:1])
-        scatter(0, part(idx2, 0), h_first[0][:], wgs_first[:, cols(0)])
-        for t in range(1, PACK):
-            codes, scales = quantize(rest_bf[:, (t - 1) * N : t * N], P, f"w1_last{t}")
-            w1_q[last, t] = (codes[:], scales[:])
-        scatter(0, part(idx2, 1), h_first[1][:], wgs_first[:, cols(1)])
-
-        h = {}
-        for t in range(1, PACK):
-            h[t] = keep.tile([P, S], F32, name=f"h{t}", tag=f"h{t}", align_bytes=64)
+        def put_halves(b):
             for u in range(HALVES):
-                nc.scalar.activation(h[t][:, cols(u)], product_h(t, u)[:], ACT.Copy, scale=gain_sb[:, t : t + 1])
+                h = keep.tile([P, N], F32, name=f"h{b}_{u}", tag=f"h{b}_{u}", align_bytes=64)
+                features(b, u, h[:])
+                nc.vector.tensor_tensor(pages[b][:].indirect(part(idx2, u)), h[:], wgs_sb[:, cols(u)], ALU.mult)
 
-        x = [keep.tile([P, PACK, N], F32, name=f"x{u}") for u in range(HALVES)]
-
-        def scale_missed(t, u, source):
-            nc.scalar.activation(x[u][:, t, :], source, ACT.Copy, scale=miss_sb[:, t : t + 1])
-
-        def gather_missed(t):
-            missed = ring.tile([P, M], F32, name="missed", tag="big")
-            nc.vector.tensor_copy(missed[:], pages[t][:].indirect(idx3[:]))
+        def put_whole(b):
+            h = keep.tile([P, S], F32, name=f"h{b}", tag=f"h{b}", align_bytes=64)
             for u in range(HALVES):
-                scale_missed(t, u, missed[:, cols(u)])
+                features(b, u, h[:, cols(u)])
+            nc.vector.tensor_tensor(pages[b][:].indirect(idx2[:]), h[:], wgs_sb[:], ALU.mult)
 
-        def gather_missed_half(t, u):
-            missed = ring.tile([P, N], F32, name="missed_half", tag="big")
-            nc.vector.tensor_copy(missed[:], pages[t][:].indirect(part(idx3, u)))
+        def reread(b, tag):
+            missed = keep.tile([P, M], F32, name=f"missed{b}", tag=tag, align_bytes=64)
+            nc.vector.tensor_copy(missed[:], pages[b][:].indirect(idx3[:]))
             return missed
+
+        def scale_missed(b, missed):
+            scaled = keep.tile([P, M], F32, name=f"scaled{b}", tag=f"gain{b + 1}")
+            nc.scalar.activation(scaled[:], missed[:], ACT.Copy, scale=miss_sb[:, b : b + 1])
+            return scaled
+
+        def deal(b, scaled):
+            for j in range(PACK):
+                nc.sync.dma_start(
+                    out=x[QUAD * b : QUAD * (b + 1), :, j, :],
+                    in_=scaled[j::PACK, :].rearrange("q (u m) -> q u m", u=HALVES),
+                )
+
+        def reread_half(b, u):
+            missed = keep.tile([P, N], F32, name=f"missed{b}_{u}")
+            nc.vector.tensor_copy(missed[:], pages[b][:].indirect(part(idx3, u)))
+            scaled = keep.tile([P, N], F32, name=f"scaled{b}_{u}")
+            nc.scalar.activation(scaled[:], missed[:], ACT.Copy, scale=miss_sb[:, b : b + 1])
+            for j in range(PACK):
+                nc.sync.dma_start(out=x[QUAD * b : QUAD * (b + 1), u, j, :], in_=scaled[j::PACK, :])
 
         def signed_part(u, sign, name):
             grouped = keep.tile([P, N * PACK], BF16, name=name, tag=name, align_bytes=64)
-            nc.scalar.activation(
-                grouped[:].rearrange("p (c i t) -> p c t i", i=4, t=PACK),
-                x[u][:].rearrange("p t (c i) -> p c t i", i=4),
-                ACT.Relu,
-                scale=sign,
-            )
+            interleave(grouped[:], x[:, u, :, :], ACT.Relu, sign)
             return quantize(grouped[:], N, name)
 
         strokes = {}
 
-        def gather_model(ts, u, tag):
-            pair = keep.tile([P, M], F32, name="strokes_" + tag, tag=tag, align_bytes=64)
-            for i, t in enumerate(ts):
-                nc.vector.tensor_copy(pair[:, cols(i)], pages[t][:].indirect(part(idx4, u)))
-                strokes[t, u] = pair[:, cols(i)]
+        def gather_model(pieces, tag):
+            picked = keep.tile([P, len(pieces) * N], F32, name="strokes_" + tag, tag=tag, align_bytes=64)
+            for i, (b, u) in enumerate(pieces):
+                nc.vector.tensor_copy(picked[:, cols(i)], pages[b][:].indirect(part(idx4, u)))
+                strokes[b, u] = picked[:, cols(i)]
 
-        scatter(1, idx2[:], h[1][:], wgs_of(1))
-        gather_missed(0)
-        scatter(2, idx2[:], h[2][:], wgs_of(2))
-        gather_missed(1)
-        wn_codes, wn_scales = quantize(cast_whole(wn_raw)[:], H, "wn")
-        gather_missed(2)
-        scatter(3, idx2[:], h[3][:], wgs_of(3))
-        missed_last = [gather_missed_half(3, u) for u in range(HALVES)]
+        xq = {}
 
-        out_rows = out.rearrange("(p t) m -> p t m", t=PACK)
-
-        def larger(t, u):
+        def larger(b, u):
             (xp_c, xp_s), (xn_c, xn_s) = xq[u]
             yn = psum.tile([P, N], F32, name="yn", tag="acc")
             nc.tensor.matmul_mx(
                 out=yn[:],
-                lhsT=wn_codes[:, t * P : (t + 1) * P].bitcast(FP8X4),
-                lhsT_scale=wn_scales[:, t * P : (t + 1) * P],
+                lhsT=wn_codes[:, rows(b)].bitcast(FP8X4),
+                lhsT_scale=wn_scales[:, rows(b)],
                 rhs=xn_c[:].bitcast(FP8X4),
                 rhs_scale=xn_s[:],
                 start=True,
@@ -263,45 +256,64 @@ def tile_list_stroke_page_coaching_kernel(
             yp = psum.tile([P, N], F32, name="yp", tag="acc")
             nc.tensor.matmul_mx(
                 out=yp[:],
-                lhsT=wp_codes[:, 2 * t * P : 2 * (t + 1) * P].bitcast(FP4X4),
-                lhsT_scale=wp_sc[:, t * P : (t + 1) * P],
+                lhsT=wp_codes[:, 2 * b * P : 2 * (b + 1) * P].bitcast(FP4X4),
+                lhsT_scale=wp_sc[:, rows(b)],
                 rhs=xp_c[:].bitcast(FP8X4),
                 rhs_scale=xp_s[:],
                 start=True,
                 stop=True,
             )
-            yn_sb = ring.tile([P, N], F32, name="yn_sb", tag="picked", align_bytes=64)
+            yn_sb = ring.tile([P, N], F32, name="yn_sb", tag="yn_sb")
             nc.scalar.activation(yn_sb[:], yn[:], ACT.Copy, scale=-1.0)
             y = ring.tile([P, N], F32, name="y", tag="y")
             nc.vector.tensor_tensor(y[:], yp[:], yn_sb[:], ALU.max)
             return y
 
-        def finish(t, u, y):
+        def finish(b, u, y):
             res = ring.tile([P, N], F32, name="res", tag="res")
-            nc.vector.scalar_tensor_tensor(
-                res[:], strokes[t, u], model_sb[:, t : t + 1], y[:], ALU.mult, ALU.add
-            )
-            nc.sync.dma_start(out=out_rows[:, t, cols(u)], in_=res[:])
+            nc.vector.scalar_tensor_tensor(res[:], strokes[b, u], model_sb[:, b : b + 1], y[:], ALU.mult, ALU.add)
+            nc.sync.dma_start(out=out[rows(b), cols(u)], in_=res[:])
 
         def results(u):
             waiting = None
-            for t in range(PACK):
-                y = larger(t, u)
+            for b in range(BLOCKS):
+                y = larger(b, u)
                 if waiting is not None:
                     finish(*waiting)
-                waiting = (t, u, y)
+                waiting = (b, u, y)
             finish(*waiting)
 
-        xq = {}
-        scale_missed(3, 0, missed_last[0][:])
-        gather_model((0, 1), 0, "h3")
+        for u in range(HALVES):
+            gather_last(u)
+        put_halves(0)
+        quantize_w1(1)
+        missed = reread(0, "w1_bf1")
+        put_halves(1)
+        first = scale_missed(0, missed)
+        quantize_w1(2)
+        quantize_w1(3)
+        missed = reread(1, "w1_bf3")
+        put_halves(2)
+        wn_bf = keep.tile([P, H * PACK], BF16, name="wn_bf", tag="tab2", align_bytes=64)
+        interleave(wn_bf[:], wn_raw[:], ACT.Copy, 1.0)
+        x = keep.tile([P, HALVES, PACK, N], F32, name="x", tag="tab1", align_bytes=64)
+        deal(0, first)
+        deal(1, scale_missed(1, missed))
+        wn_codes, wn_scales = quantize(wn_bf[:], H, "wn", "h2_1")
+        missed = reread(2, "w1_bf2")
+        put_whole(3)
+        deal(2, scale_missed(2, missed))
+
+        for u in range(HALVES):
+            reread_half(3, u)
+        gather_model([(0, 0), (1, 0)], "h3")
+        gather_model([(3, 0), (3, 1)], "strokes3")
         xp = signed_part(0, 1.0, "xp0")
-        gather_model((2, 3), 0, "xp0")
+        gather_model([(2, 0), (0, 1)], "xp0")
         xq[0] = (xp, signed_part(0, -1.0, "xn0"))
-        gather_model((0, 1), 1, "xn0")
-        scale_missed(3, 1, missed_last[1][:])
+        gather_model([(1, 1)], "xn0")
         xp = signed_part(1, 1.0, "xp1")
         results(0)
         xq[1] = (xp, signed_part(1, -1.0, "xn1"))
-        gather_model((2, 3), 1, "xn1")
+        gather_model([(2, 1)], "xn1")
         results(1)

from contextlib import ExitStack

import concourse.mybir as mybir

K, H, T, S, T2, M = 1536, 512, 4096, 1024, 2048, 1024
FLOPS = 2 * K * H * S + 2 * 2 * H * H * M

F32 = mybir.dt.float32
BF16 = mybir.dt.bfloat16
I32 = mybir.dt.int32
U32 = mybir.dt.uint32
U16 = mybir.dt.uint16
U8 = mybir.dt.uint8
FP8X4 = mybir.dt.float8_e4m3fn_x4
FP4X4 = mybir.dt.float4_e2m1fn_x4
ALU = mybir.AluOpType
ACT = mybir.ActivationFunctionType

P = 128
PACK = 4
PASSES = K // (P * PACK)
BLOCKS = H // P
N = 512
HALVES = S // N
QUAD = 32
LIST_COLS = N // 16


def tile_list_stroke_page_coaching_kernel(
    tc, tab_words, tab_scales, offs, offs2, offs3, offs4, w1, gain, wgs, page0, miss,
    wp_words, wp_scales, wn, model, out,
):
    nc = tc.nc
    with ExitStack() as ctx:
        lists = ctx.enter_context(tc.tile_pool(name="lists", bufs=1))
        keep = ctx.enter_context(tc.tile_pool(name="keep", bufs=1))
        ring = ctx.enter_context(tc.tile_pool(name="ring", bufs=3))
        psum = ctx.enter_context(tc.psum_pool(name="psum", bufs=8))

        def cols(u):
            return slice(u * N, (u + 1) * N)

        def rows(b):
            return slice(b * P, (b + 1) * P)

        def part(lst, u):
            return lst[:, u * LIST_COLS : (u + 1) * LIST_COLS]

        idx1 = lists.tile([P, S // 16], U16, name="idx1")
        idx2 = lists.tile([P, S // 16], U16, name="idx2")
        idx3 = lists.tile([P, M // 16], U16, name="idx3")
        idx4 = lists.tile([P, M // 16], U16, name="idx4")

        tab_sc = keep.tile([P, T], U8, name="tab_sc", align_bytes=64)
        wp_sc = keep.tile([P, H], U8, name="wp_sc", align_bytes=64)
        wp_codes = keep.tile([P, 2 * H], U8, name="wp_codes", align_bytes=64)
        gains = [keep.tile([P, 1], F32, name=f"gain{b}", tag=f"gain{b}") for b in range(BLOCKS)]
        miss_sb = keep.tile([P, BLOCKS], F32, name="miss_sb")
        model_sb = keep.tile([P, BLOCKS], F32, name="model_sb")
        pages = [keep.tile([P, T2], F32, name=f"page{b}") for b in range(BLOCKS)]
        wgs_sb = keep.tile([P, S], F32, name="wgs_sb")

        nc.vector.memset(tab_sc[:].bitcast(I32), 0)
        nc.vector.memset(wp_sc[:].bitcast(I32), 0)

        def load_tab(a):
            tab = keep.tile([P, T], I32, name=f"tab{a}", tag=f"tab{a}", align_bytes=64)
            nc.sync.dma_start(out=tab[:], in_=tab_words[a].rearrange("p t i -> p (t i)").bitcast(I32))
            return tab

        def load_weight(weight, tag):
            raw = keep.tile([P, PACK, weight.shape[1]], F32, name="raw_" + tag, tag=tag, align_bytes=64)
            nc.sync.dma_start(out=raw[:], in_=weight.rearrange("(p j) c -> p j c", j=PACK))
            return raw

        def load_w1(a, b0, b1):
            raw = load_weight(w1[a * P * PACK : (a + 1) * P * PACK, b0 * P : b1 * P], f"w1_raw{a}_{b0}")
            for b in range(b0, b1):
                w1_raw[a, b] = raw[:, :, rows(b - b0)]

        def load_vector(tile, vec):
            with nc.allow_non_contiguous_dma(reason="one value of a row vector to each partition"):
                nc.sync.dma_start(out=tile[:], in_=vec.rearrange("(b p) -> p b", p=P))

        def load_gain(b):
            with nc.allow_non_contiguous_dma(reason="one value of a row vector to each partition"):
                nc.sync.dma_start(out=gains[b][:], in_=gain[rows(b)].rearrange("(p o) -> p o", o=1))

        def load_page(b):
            nc.sync.dma_start(out=pages[b][:], in_=page0[rows(b), :])

        w1_raw = {}
        nc.sync.dma_start(idx1[:], offs)
        tabs = [load_tab(0)]
        for q in range(4):
            nc.sync.dma_start(
                out=tab_sc[QUAD * q : QUAD * q + 4 * PASSES, :].bitcast(I32),
                in_=tab_scales[:, 4 * q : 4 * q + 4, :].bitcast(I32),
            )
        load_w1(0, 0, 1)
        load_w1(1, 0, 1)
        tabs.append(load_tab(1))
        load_w1(2, 0, 1)
        load_gain(0)
        nc.sync.dma_start(idx2[:], offs2)
        tabs.append(load_tab(2))
        load_page(0)
        for u in range(HALVES):
            nc.sync.dma_start(out=wgs_sb[:, cols(u)], in_=wgs[:, cols(u)])
        for a in range(PASSES):
            load_w1(a, 1, 2)
        load_gain(1)
        load_vector(miss_sb, miss)
        nc.sync.dma_start(idx3[:], offs3)
        load_page(1)
        for a in range(PASSES):
            load_w1(a, 2, BLOCKS)
        load_gain(2)
        wn_raw = load_weight(wn, "tab1")
        load_page(2)
        load_gain(3)
        load_page(3)
        nc.sync.dma_start(idx4[:], offs4)
        nc.sync.dma_start(out=wp_codes[:].bitcast(I32), in_=wp_words[0].bitcast(I32))
        for q in range(4):
            nc.sync.dma_start(
                out=wp_sc[QUAD * q : QUAD * q + 4, :].bitcast(I32),
                in_=wp_scales[0, 4 * q : 4 * q + 4, :].bitcast(I32),
            )
        load_vector(model_sb, model)

        def interleave(grouped, source, func, scale):
            nc.scalar.activation(
                grouped.rearrange("p (c i j) -> p c j i", i=4, j=PACK),
                source.rearrange("p j (c i) -> p c j i", i=4),
                func,
                scale=scale,
            )

        def quantize(grouped, width, name, codes_tag=None):
            codes = keep.tile([P, width], U32, name=name + "_codes", tag=codes_tag or name + "_codes", align_bytes=64)
            scales = keep.tile([P, width], U8, name=name + "_scales", align_bytes=64)
            nc.vector.quantize_mx(out=codes[:].bitcast(FP8X4), scales=scales[:], in_=grouped)
            return codes, scales

        w1_q = {}

        def quantize_w1(b):
            grouped = keep.tile([P, PASSES * P * PACK], BF16, name=f"w1_bf{b}", tag=f"w1_bf{b}", align_bytes=64)
            for a in range(PASSES):
                interleave(grouped[:, cols(a)], w1_raw[a, b], ACT.Copy, 1.0)
            codes, scales = quantize(grouped[:, : 2 * N], 2 * P, f"w1_{b}_low")
            for a in range(2):
                w1_q[a, b] = (codes[:, rows(a)], scales[:, rows(a)])
            codes, scales = quantize(grouped[:, 2 * N :], P, f"w1_{b}_high")
            w1_q[2, b] = (codes[:], scales[:])

        v_codes = {}
        v_scales = keep.tile([P, S], U8, name="v_scales", align_bytes=64)
        last = PASSES - 1
        for a in range(last):
            picked = keep.tile([P, S], U32, name=f"picked{a}", align_bytes=64)
            nc.vector.tensor_copy(picked[:], tabs[a][:].bitcast(U32).indirect(idx1[:]))
            for u in range(HALVES):
                v_codes[a, u] = picked[:, cols(u)]
            if a == 0:
                nc.vector.tensor_copy(v_scales[:], tab_sc[:].indirect(idx1[:]))
                quantize_w1(0)

        def gather_last(u):
            picked = keep.tile([P, N], U32, name=f"picked_last{u}", align_bytes=64)
            nc.vector.tensor_copy(picked[:], tabs[last][:].bitcast(U32).indirect(part(idx1, u)))
            v_codes[last, u] = picked[:]

        def product_h(b, u):
            acc = psum.tile([P, N], F32, name="acc", tag="acc")
            for a in range(PASSES):
                nc.tensor.matmul_mx(
                    out=acc[:],
                    lhsT=w1_q[a, b][0].bitcast(FP8X4),
                    lhsT_scale=w1_q[a, b][1],
                    rhs=v_codes[a, u].bitcast(FP8X4),
                    rhs_scale=v_scales[4 * a :, cols(u)],
                    start=(a == 0),
                    stop=(a == last),
                )
            return acc

        def features(b, u, h):
            nc.scalar.activation(h, product_h(b, u)[:], ACT.Copy, scale=gains[b][:])

        def put_halves(b):
            for u in range(HALVES):
                h = keep.tile([P, N], F32, name=f"h{b}_{u}", tag=f"h{b}_{u}", align_bytes=64)
                features(b, u, h[:])
                nc.vector.tensor_tensor(pages[b][:].indirect(part(idx2, u)), h[:], wgs_sb[:, cols(u)], ALU.mult)

        def put_whole(b):
            h = keep.tile([P, S], F32, name=f"h{b}", tag=f"h{b}", align_bytes=64)
            for u in range(HALVES):
                features(b, u, h[:, cols(u)])
            nc.vector.tensor_tensor(pages[b][:].indirect(idx2[:]), h[:], wgs_sb[:], ALU.mult)

        def reread(b, tag):
            missed = keep.tile([P, M], F32, name=f"missed{b}", tag=tag, align_bytes=64)
            nc.vector.tensor_copy(missed[:], pages[b][:].indirect(idx3[:]))
            return missed

        def scale_missed(b, missed):
            scaled = keep.tile([P, M], F32, name=f"scaled{b}", tag=f"gain{b + 1}")
            nc.scalar.activation(scaled[:], missed[:], ACT.Copy, scale=miss_sb[:, b : b + 1])
            return scaled

        def deal(b, scaled):
            for j in range(PACK):
                nc.sync.dma_start(
                    out=x[QUAD * b : QUAD * (b + 1), :, j, :],
                    in_=scaled[j::PACK, :].rearrange("q (u m) -> q u m", u=HALVES),
                )

        def reread_half(b, u):
            missed = keep.tile([P, N], F32, name=f"missed{b}_{u}")
            nc.vector.tensor_copy(missed[:], pages[b][:].indirect(part(idx3, u)))
            scaled = keep.tile([P, N], F32, name=f"scaled{b}_{u}")
            nc.scalar.activation(scaled[:], missed[:], ACT.Copy, scale=miss_sb[:, b : b + 1])
            for j in range(PACK):
                nc.sync.dma_start(out=x[QUAD * b : QUAD * (b + 1), u, j, :], in_=scaled[j::PACK, :])

        def signed_part(u, sign, name):
            grouped = keep.tile([P, N * PACK], BF16, name=name, tag=name, align_bytes=64)
            interleave(grouped[:], x[:, u, :, :], ACT.Relu, sign)
            return quantize(grouped[:], N, name)

        strokes = {}

        def gather_model(pieces, tag):
            picked = keep.tile([P, len(pieces) * N], F32, name="strokes_" + tag, tag=tag, align_bytes=64)
            for i, (b, u) in enumerate(pieces):
                nc.vector.tensor_copy(picked[:, cols(i)], pages[b][:].indirect(part(idx4, u)))
                strokes[b, u] = picked[:, cols(i)]

        xq = {}

        def larger(b, u):
            (xp_c, xp_s), (xn_c, xn_s) = xq[u]
            yn = psum.tile([P, N], F32, name="yn", tag="acc")
            nc.tensor.matmul_mx(
                out=yn[:],
                lhsT=wn_codes[:, rows(b)].bitcast(FP8X4),
                lhsT_scale=wn_scales[:, rows(b)],
                rhs=xn_c[:].bitcast(FP8X4),
                rhs_scale=xn_s[:],
                start=True,
                stop=True,
            )
            yp = psum.tile([P, N], F32, name="yp", tag="acc")
            nc.tensor.matmul_mx(
                out=yp[:],
                lhsT=wp_codes[:, 2 * b * P : 2 * (b + 1) * P].bitcast(FP4X4),
                lhsT_scale=wp_sc[:, rows(b)],
                rhs=xp_c[:].bitcast(FP8X4),
                rhs_scale=xp_s[:],
                start=True,
                stop=True,
            )
            yn_sb = ring.tile([P, N], F32, name="yn_sb", tag="yn_sb")
            nc.scalar.activation(yn_sb[:], yn[:], ACT.Copy, scale=-1.0)
            y = ring.tile([P, N], F32, name="y", tag="y")
            nc.vector.tensor_tensor(y[:], yp[:], yn_sb[:], ALU.max)
            return y

        def finish(b, u, y):
            res = ring.tile([P, N], F32, name="res", tag="res")
            nc.vector.scalar_tensor_tensor(res[:], strokes[b, u], model_sb[:, b : b + 1], y[:], ALU.mult, ALU.add)
            nc.sync.dma_start(out=out[rows(b), cols(u)], in_=res[:])

        def results(u):
            waiting = None
            for b in range(BLOCKS):
                y = larger(b, u)
                if waiting is not None:
                    finish(*waiting)
                waiting = (b, u, y)
            finish(*waiting)

        for u in range(HALVES):
            gather_last(u)
        put_halves(0)
        quantize_w1(1)
        missed = reread(0, "w1_bf1")
        put_halves(1)
        first = scale_missed(0, missed)
        quantize_w1(2)
        quantize_w1(3)
        missed = reread(1, "w1_bf3")
        put_halves(2)
        wn_bf = keep.tile([P, H * PACK], BF16, name="wn_bf", tag="tab2", align_bytes=64)
        interleave(wn_bf[:], wn_raw[:], ACT.Copy, 1.0)
        x = keep.tile([P, HALVES, PACK, N], F32, name="x", tag="tab1", align_bytes=64)
        deal(0, first)
        deal(1, scale_missed(1, missed))
        wn_codes, wn_scales = quantize(wn_bf[:], H, "wn", "h2_1")
        missed = reread(2, "w1_bf2")
        put_whole(3)
        deal(2, scale_missed(2, missed))

        for u in range(HALVES):
            reread_half(3, u)
        gather_model([(0, 0), (1, 0)], "h3")
        gather_model([(3, 0), (3, 1)], "strokes3")
        xp = signed_part(0, 1.0, "xp0")
        gather_model([(2, 0), (0, 1)], "xp0")
        xq[0] = (xp, signed_part(0, -1.0, "xn0"))
        gather_model([(1, 1)], "xn0")
        xp = signed_part(1, 1.0, "xp1")
        results(0)
        xq[1] = (xp, signed_part(1, -1.0, "xn1"))
        gather_model([(2, 1)], "xn1")
        results(1)
